import numpy as np
import ml_dtypes


def mxq(x, axis, fmt="e4m3"):
    dtype, down = {"e4m3": (ml_dtypes.float8_e4m3fn, 7), "e5m2": (ml_dtypes.float8_e5m2, 14)}[fmt]
    v = np.moveaxis(np.asarray(x, np.float32).astype(ml_dtypes.bfloat16).astype(np.float64), axis, -1)
    blocks = v.reshape(v.shape[:-1] + (-1, 32))
    amax = np.abs(blocks).max(-1, keepdims=True)
    byte = np.maximum(np.where(amax > 0, np.frexp(amax)[1] - 1 + 127, 0) - down, 1)
    scale = np.exp2(byte - 127.0)
    codes = (blocks / scale).astype(np.float32).astype(dtype).astype(np.float64)
    return np.moveaxis((codes * scale).reshape(v.shape), -1, axis)


WIDE = False


def mx_kscale(k):
    if not WIDE:
        return np.ones(k)
    levels = np.array([10, -10, 5, -5, 0])
    if k % 512:
        return np.exp2(np.random.permutation(np.resize(levels, k // 32))).repeat(32)
    a = np.empty((k // 512, 16))
    for p in range(k // 512):
        a[p, :8] = np.random.permutation(np.resize(levels, 8))
        for g in range(8):
            far = levels[np.abs(levels - a[p, g]) >= 10]
            a[p, g + 8] = far[np.random.randint(len(far))]
    return np.exp2(a.ravel()).repeat(32)


def f64(x):
    return np.asarray(x).astype(np.float64)


def striped(idx):
    return np.tile(idx.reshape(-1, 16).T, (8, 1)).astype(np.uint16)


def unstriped(offs):
    return offs[:16].T.reshape(-1).astype(np.int64)


E2M1 = np.array([0.0, 0.5, 1.0, 1.5, 2.0, 3.0, 4.0, 6.0, -0.0, -0.5, -1.0, -1.5, -2.0, -3.0, -4.0, -6.0])


def pack_weight(w, fmt):
    k, n = w.shape
    w = f64(np.asarray(w, np.float32).astype(ml_dtypes.bfloat16)).reshape(k // 32, 32, n)
    amax = np.abs(w).max(1)
    if fmt == "e4m3":
        byte = np.frexp(amax)[1] - 1 + 127 - 7
    else:
        mant, ex = np.frexp(amax / 6.0)
        byte = np.where(mant > 0.5, ex, ex - 1) + 127
    byte = np.clip(np.where(amax > 0, byte, 1), 1, 254)
    scaled = (w * np.exp2(127.0 - byte)[:, None, :]).reshape(k, n).astype(np.float32)
    by_word = np.ascontiguousarray(scaled.reshape(k // 512, 128, 4, n).transpose(0, 1, 3, 2))
    if fmt == "e4m3":
        words = by_word.astype(ml_dtypes.float8_e4m3fn).view(np.uint8)
    else:
        c = by_word.astype(ml_dtypes.float4_e2m1fn).view(np.uint8) & 0xF
        words = (c[..., 0::2] | (c[..., 1::2] << 4)).reshape(k // 512, 128, 2 * n)
    return np.ascontiguousarray(words), np.ascontiguousarray(byte.astype(np.uint8).reshape(k // 512, 16, n))


def unpack_weight(words, scales, fmt):
    g, _, n = scales.shape
    words = np.ascontiguousarray(words).reshape(g, 128, n, -1)
    if fmt == "e4m3":
        vals = words.view(ml_dtypes.float8_e4m3fn).astype(np.float64)
    else:
        nib = np.empty((g, 128, n, 4), np.uint8)
        nib[..., 0::2] = words & 0xF
        nib[..., 1::2] = words >> 4
        vals = E2M1[nib]
    vals = vals * np.repeat(np.exp2(scales.astype(np.float64) - 127.0), 8, axis=1)[..., None]
    return vals.transpose(0, 1, 3, 2).reshape(g * 512, n)


def gelu(v):
    return 0.5 * v * (1.0 + np.tanh(np.sqrt(2.0 / np.pi) * (v + 0.044715 * v**3)))


K, T, S, H, T2, P, N = 1536, 4096, 1024, 512, 2048, 512, 768


def setup_inputs():
    n = np.random.standard_normal
    s = mx_kscale(K)[:, None]
    u = mx_kscale(H)[:, None]
    tab_words, tab_scales = pack_weight(n((K, T)) * s, "e4m3")
    w4_words, w4_scales = pack_weight(n((H, N)) / np.sqrt(H) / u, "e2m1")
    perm = np.random.permutation(T2)
    return {
        "tab_words": tab_words, "tab_scales": tab_scales,
        "w1": (1.6 * n((K, H)) / np.sqrt(K) / s).astype(np.float32),
        "gain": (1.2 * np.exp(0.3 * n(H)) * u[:, 0]).astype(np.float32),
        "wgs": np.exp(0.3 * n((128, S))).astype(np.float32),
        "page0": (n((H, T2)) * u).astype(np.float32),
        "conf": (0.6 * np.exp(0.3 * n(H))).astype(np.float32),
        "w4_words": w4_words, "w4_scales": w4_scales,
        "offs": striped(np.random.permutation(T)[:S]),
        "offs2": striped(np.random.permutation(T2)[:S]),
        "offs3": striped(perm[:P]),
        "offs4": striped(perm[P:2 * P]),
    }


def reference(tab_words, tab_scales, w1, gain, wgs, page0, conf, w4_words, w4_scales, offs, offs2, offs3, offs4):
    v = unpack_weight(tab_words, tab_scales, "e4m3")[:, unstriped(offs)]
    w4 = unpack_weight(w4_words, w4_scales, "e2m1")
    x = mxq(f64(w1), 0, "e4m3").T @ v
    h = f64(gain)[:, None] * (x / (1.0 + np.exp(-x)))
    page = f64(page0).copy()
    page[:, unstriped(offs2)] = np.tile(f64(wgs), (H // 128, 1)) * h
    a = page[:, unstriped(offs3)]
    b = page[:, unstriped(offs4)]
    d = f64(conf)[:, None] * np.abs(a - b)
    page[:, unstriped(offs3)] = a + d
    page[:, unstriped(offs4)] = b - d
    y = w4.T @ mxq(page, 0, "e4m3")
    return y

@@ -1,0 +1,227 @@
+from contextlib import ExitStack
+
+import concourse.mybir as mybir
+
+K, T, S, H, T2, PAIRS, N = 1536, 4096, 1024, 512, 2048, 512, 768
+FLOPS = 2 * K * H * S + 2 * H * N * T2
+
+F32 = mybir.dt.float32
+BF16 = mybir.dt.bfloat16
+I32 = mybir.dt.int32
+U32 = mybir.dt.uint32
+U16 = mybir.dt.uint16
+U8 = mybir.dt.uint8
+FP8X4 = mybir.dt.float8_e4m3fn_x4
+FP4X4 = mybir.dt.float4_e2m1fn_x4
+ALU = mybir.AluOpType
+ACT = mybir.ActivationFunctionType
+
+P = 128
+PACK = 4
+PASSES = K // (P * PACK)
+HALF = S // 2
+CHUNKS = [256, 256, 512, 512, 512]
+BANK = 512
+
+
+def tile_list_roundabout_entry_scores_kernel(
+    tc, tab_words, tab_scales, w1, gain, wgs, page0, conf, w4_words, w4_scales, offs, offs2, offs3, offs4, out
+):
+    nc = tc.nc
+    with ExitStack() as ctx:
+        lists = ctx.enter_context(tc.tile_pool(name="lists", bufs=1))
+        keep = ctx.enter_context(tc.tile_pool(name="keep", bufs=1))
+        psum = ctx.enter_context(tc.psum_pool(name="psum", bufs=8))
+
+        idx = lists.tile([P, S // 16], U16, name="idx")
+        idx2 = lists.tile([P, S // 16], U16, name="idx2")
+        idx3 = lists.tile([P, PAIRS // 16], U16, name="idx3")
+        idx4 = lists.tile([P, PAIRS // 16], U16, name="idx4")
+
+        gain_sb = keep.tile([P, PACK], F32, name="gain_sb")
+        conf_sb = keep.tile([P, PACK], F32, name="conf_sb")
+        pages = [keep.tile([P, T2], F32, name=f"page{t}") for t in range(PACK)]
+        wgs_sb = [keep.tile([P, S], F32, name=f"wgs{t}") for t in range(PACK)]
+        h = [keep.tile([P, S], F32, name=f"h{t}") for t in range(PACK)]
+        w4_codes = keep.tile([P, 2 * N], U8, name="w4_codes", align_bytes=64)
+        w4_plane = keep.tile([P, N], U8, name="w4_plane", align_bytes=64)
+        v_codes = [keep.tile([P, S], U32, name=f"v_codes{a}", align_bytes=64) for a in range(PASSES - 1)]
+        tab_planes = keep.tile([P, T], U8, name="tab_planes", tag="planes_then_codes", align_bytes=64)
+        v_planes = keep.tile([P, S], U8, name="v_planes", align_bytes=64)
+        w1_codes = [keep.tile([P, H], U32, name=f"w1_codes{a}", align_bytes=64) for a in range(PASSES)]
+        w1_plane = [keep.tile([P, H], U8, name=f"w1_plane{a}", align_bytes=64) for a in range(PASSES)]
+
+        def load_slice(t):
+            for q in range(4):
+                nc.sync.dma_start(out=wgs_sb[t][32 * q : 32 * q + 32, :], in_=wgs.rearrange("(q t) j -> t q j", t=PACK)[t])
+            nc.sync.dma_start(out=pages[t][:], in_=page0.rearrange("(p t) c -> t p c", t=PACK)[t])
+
+        with tc.tile_pool(name="head", bufs=1) as head:
+            tab_sb = [head.tile([P, T], U32, name=f"tab{a}", align_bytes=64) for a in range(PASSES)]
+            w1_raw = [head.tile([P, PACK, H], F32, name=f"w1_raw{a}") for a in range(PASSES)]
+            w1_bf = [head.tile([P, PACK * H], BF16, name=f"w1_bf{a}", align_bytes=64) for a in range(PASSES)]
+
+            nc.vector.memset(tab_planes[:].bitcast(I32), 0)
+            nc.vector.memset(w4_plane[:].bitcast(I32), 0)
+            for q in range(4):
+                nc.gpsimd.dma_start(
+                    out=tab_planes[32 * q : 32 * q + 4 * PASSES, :].bitcast(I32),
+                    in_=tab_scales[:, 4 * q : 4 * q + 4, :].bitcast(I32),
+                )
+            for a in range(PASSES):
+                nc.sync.dma_start(out=w1_raw[a][:], in_=w1[512 * a : 512 * (a + 1), :].rearrange("(p j) c -> p j c", j=PACK))
+            nc.sync.dma_start(idx[:], offs)
+            for a in range(PASSES):
+                nc.sync.dma_start(
+                    out=tab_sb[a][:].bitcast(I32), in_=tab_words[a].rearrange("p t i -> p (t i)").bitcast(I32)
+                )
+            nc.sync.dma_start(out=gain_sb[:], in_=gain.rearrange("(p t) -> p t", t=PACK))
+            nc.sync.dma_start(idx2[:], offs2)
+            for t in range(PACK):
+                load_slice(t)
+            nc.sync.dma_start(idx3[:], offs3)
+            nc.sync.dma_start(idx4[:], offs4)
+            nc.sync.dma_start(out=conf_sb[:], in_=conf.rearrange("(p t) -> p t", t=PACK))
+            nc.sync.dma_start(out=w4_codes[:].bitcast(I32), in_=w4_words[0].bitcast(I32))
+            for q in range(4):
+                nc.sync.dma_start(
+                    out=w4_plane[32 * q : 32 * q + 4, :].bitcast(I32),
+                    in_=w4_scales[0, 4 * q : 4 * q + 4, :].bitcast(I32),
+                )
+
+            for a in range(PASSES):
+                nc.scalar.copy(
+                    out=w1_bf[a][:].rearrange("p (t m j) -> p m t j", t=PACK, j=PACK),
+                    in_=w1_raw[a][:].rearrange("p j (m t) -> p m t j", t=PACK),
+                )
+                nc.vector.quantize_mx(out=w1_codes[a][:].bitcast(FP8X4), scales=w1_plane[a][:], in_=w1_bf[a][:])
+
+            nc.vector.tensor_copy(v_planes[:], tab_planes[:].indirect(idx[:]))
+            for a in range(PASSES - 1):
+                nc.vector.tensor_copy(v_codes[a][:], tab_sb[a][:].indirect(idx[:]))
+            v_codes.append(keep.tile([P, S], U32, name="v_codes_last", tag="planes_then_codes", align_bytes=64))
+            for u in range(2):
+                nc.vector.tensor_copy(
+                    v_codes[PASSES - 1][:, HALF * u : HALF * (u + 1)],
+                    tab_sb[PASSES - 1][:].indirect(idx[:, 32 * u : 32 * (u + 1)]),
+                )
+
+        with tc.tile_pool(name="tail", bufs=1) as tail:
+            for t in range(PACK):
+                for u in range(2):
+                    cols = slice(HALF * u, HALF * (u + 1))
+                    x = psum.tile([P, BANK], F32, name="bank")
+                    for a in range(PASSES):
+                        nc.tensor.matmul_mx(
+                            out=x[:],
+                            lhsT=w1_codes[a][:, P * t : P * (t + 1)].bitcast(FP8X4),
+                            lhsT_scale=w1_plane[a][:, P * t : P * (t + 1)],
+                            rhs=v_codes[a][:, cols].bitcast(FP8X4),
+                            rhs_scale=v_planes[4 * a :, cols],
+                            start=(a == 0),
+                            stop=(a == PASSES - 1),
+                        )
+                    act = tail.tile([P, HALF], F32, name="act", bufs=2)
+                    nc.scalar.activation(act[:], x[:], ACT.Silu)
+                    nc.scalar.activation(h[t][:, cols], act[:], ACT.Copy, scale=gain_sb[:, t : t + 1])
+                    if t == 0:
+                        nc.vector.tensor_tensor(
+                            pages[t][:].indirect(idx2[:, 32 * u : 32 * (u + 1)]), h[t][:, cols], wgs_sb[t][:, cols], ALU.mult
+                        )
+                if t > 0:
+                    nc.vector.tensor_tensor(pages[t][:].indirect(idx2[:]), h[t][:], wgs_sb[t][:], ALU.mult)
+
+            arm_a = [tail.tile([P, PAIRS], F32, name=f"arm_a{t}") for t in range(PACK)]
+            arm_b = [tail.tile([P, PAIRS], F32, name=f"arm_b{t}") for t in range(PACK)]
+            diff = [tail.tile([P, PAIRS], F32, name=f"diff{t}") for t in range(PACK)]
+            gap = [tail.tile([P, PAIRS], F32, name=f"gap{t}") for t in range(PACK)]
+            neg_gap = [tail.tile([P, PAIRS], F32, name=f"neg_gap{t}") for t in range(PACK)]
+            starts = [sum(CHUNKS[:c]) for c in range(len(CHUNKS))]
+            b_rows = [tail.tile([P, PACK, w], BF16, name=f"b_rows{c}", align_bytes=64) for c, w in enumerate(CHUNKS)]
+
+            def fetch_a(t):
+                nc.vector.tensor_copy(arm_a[t][:], pages[t][:].indirect(idx3[:]))
+
+            def fetch_b(t):
+                nc.vector.tensor_copy(arm_b[t][:], pages[t][:].indirect(idx4[:]))
+
+            def gaps(t):
+                nc.vector.tensor_tensor(diff[t][:], arm_a[t][:], arm_b[t][:], ALU.subtract)
+                nc.scalar.activation(gap[t][:], diff[t][:], ACT.Abs, scale=conf_sb[:, t : t + 1])
+                nc.scalar.activation(neg_gap[t][:], gap[t][:], ACT.Copy, scale=-1.0)
+
+            def put_a(t):
+                nc.vector.tensor_tensor(pages[t][:].indirect(idx3[:]), arm_a[t][:], gap[t][:], ALU.add)
+
+            def put_b(t):
+                nc.vector.tensor_tensor(pages[t][:].indirect(idx4[:]), arm_b[t][:], neg_gap[t][:], ALU.add)
+
+            def round_slot(t, c):
+                nc.scalar.copy(out=b_rows[c][:, t, :], in_=pages[t][:, starts[c] : starts[c] + CHUNKS[c]])
+
+            def round_slice(t):
+                for c in range(len(CHUNKS)):
+                    round_slot(t, c)
+
+            fetch_a(0)
+            fetch_b(0)
+            fetch_a(1)
+            gaps(0)
+            fetch_b(1)
+            fetch_a(2)
+            put_a(0)
+            gaps(1)
+            put_b(0)
+            fetch_b(2)
+            put_a(1)
+            gaps(2)
+            round_slice(0)
+            put_b(1)
+            fetch_a(3)
+            fetch_b(3)
+            put_a(2)
+            gaps(3)
+            round_slice(1)
+            put_b(2)
+            round_slice(2)
+            put_a(3)
+            put_b(3)
+            round_slice(3)
+
+            out_blocks = out.rearrange("(b p) c -> p b c", p=P)
+            for c, w in enumerate(CHUNKS):
+                b_bf = tail.tile([P, w, PACK], BF16, name=f"b_bf{c}", align_bytes=64)
+                nc.vector.tensor_copy(
+                    out=b_bf[:].rearrange("p (c i) t -> p c t i", i=4),
+                    in_=b_rows[c][:].rearrange("p t (c i) -> p c t i", i=4),
+                )
+                b_codes = tail.tile([P, w], U32, name=f"b_codes{c}", align_bytes=64)
+                b_plane = tail.tile([P, w], U8, name=f"b_plane{c}", align_bytes=64)
+                nc.vector.quantize_mx(
+                    out=b_codes[:].bitcast(FP8X4), scales=b_plane[:], in_=b_bf[:].rearrange("p w t -> p (w t)")
+                )
+                per_bank = BANK // w
+                for g in range(N // P // 2):
+                    staged = tail.tile([P, 2, w], F32, name="staged", bufs=6)
+                    for s in range(2 // per_bank):
+                        y = psum.tile([P, per_bank, w], F32, name="bank")
+                        for i in range(per_bank):
+                            b = 2 * g + per_bank * s + i
+                            nc.tensor.matmul_mx(
+                                out=y[:, i, :],
+                                lhsT=w4_codes[:, 2 * P * b : 2 * P * (b + 1)].bitcast(FP4X4),
+                                lhsT_scale=w4_plane[:, P * b : P * (b + 1)],
+                                rhs=b_codes[:].bitcast(FP8X4),
+                                rhs_scale=b_plane[:],
+                                start=True,
+                                stop=True,
+                            )
+                        dst = staged[:, per_bank * s : per_bank * (s + 1), :]
+                        bank_no = g * (2 // per_bank) + s
+                        if c >= len(CHUNKS) - 2 and bank_no % 2 == 1:
+                            nc.vector.tensor_copy(out=dst, in_=y[:])
+                        else:
+                            nc.scalar.copy(out=dst, in_=y[:])
+                    nc.sync.dma_start(
+                        out=out_blocks[:, 2 * g : 2 * g + 2, starts[c] : starts[c] + w], in_=staged[:]
+                    )

@@ -1,6 +1,7 @@
 from contextlib import ExitStack
 
 import concourse.mybir as mybir
+from concourse.masks import make_identity
 
 K, T, S, H, T2, PAIRS, N = 1536, 4096, 1024, 512, 2048, 512, 768
 FLOPS = 2 * K * H * S + 2 * H * N * T2
@@ -31,7 +32,7 @@ def tile_list_roundabout_entry_scores_kernel(
     with ExitStack() as ctx:
         lists = ctx.enter_context(tc.tile_pool(name="lists", bufs=1))
         keep = ctx.enter_context(tc.tile_pool(name="keep", bufs=1))
-        psum = ctx.enter_context(tc.psum_pool(name="psum", bufs=8))
+        psum = ctx.enter_context(tc.psum_pool(name="psum", bufs=1))
 
         idx = lists.tile([P, S // 16], U16, name="idx")
         idx2 = lists.tile([P, S // 16], U16, name="idx2")
@@ -41,8 +42,9 @@ def tile_list_roundabout_entry_scores_kernel(
         gain_sb = keep.tile([P, PACK], F32, name="gain_sb")
         conf_sb = keep.tile([P, PACK], F32, name="conf_sb")
         pages = [keep.tile([P, T2], F32, name=f"page{t}") for t in range(PACK)]
-        wgs_sb = [keep.tile([P, S], F32, name=f"wgs{t}") for t in range(PACK)]
-        h = [keep.tile([P, S], F32, name=f"h{t}") for t in range(PACK)]
+        pieces = [(0, 0, HALF), (0, HALF, HALF)] + [(t, 0, S) for t in range(1, PACK)]
+        wgs_sb = {(t, j0): keep.tile([P, n], F32, name=f"wgs{t}_{j0}") for t, j0, n in pieces}
+        weight = {(t, j0): keep.tile([P, n], F32, name=f"weight{t}_{j0}") for t, j0, n in pieces}
         w4_codes = keep.tile([P, 2 * N], U8, name="w4_codes", align_bytes=64)
         w4_plane = keep.tile([P, N], U8, name="w4_plane", align_bytes=64)
         v_codes = [keep.tile([P, S], U32, name=f"v_codes{a}", align_bytes=64) for a in range(PASSES - 1)]
@@ -51,10 +53,19 @@ def tile_list_roundabout_entry_scores_kernel(
         w1_codes = [keep.tile([P, H], U32, name=f"w1_codes{a}", align_bytes=64) for a in range(PASSES)]
         w1_plane = [keep.tile([P, H], U8, name=f"w1_plane{a}", align_bytes=64) for a in range(PASSES)]
 
-        def load_slice(t):
+        ident = keep.tile([P, P], F32, name="ident")
+        make_identity(nc, ident[:])
+
+        def load_wgs(t, j0, n):
             for q in range(4):
-                nc.sync.dma_start(out=wgs_sb[t][32 * q : 32 * q + 32, :], in_=wgs.rearrange("(q t) j -> t q j", t=PACK)[t])
+                nc.sync.dma_start(
+                    out=wgs_sb[t, j0][32 * q : 32 * q + 32, :],
+                    in_=wgs.rearrange("(q t) j -> t q j", t=PACK)[t][:, j0 : j0 + n],
+                )
+
+        def load_page(t):
             nc.sync.dma_start(out=pages[t][:], in_=page0.rearrange("(p t) c -> t p c", t=PACK)[t])
+
 
         with tc.tile_pool(name="head", bufs=1) as head:
             tab_sb = [head.tile([P, T], U32, name=f"tab{a}", align_bytes=64) for a in range(PASSES)]
@@ -63,22 +74,28 @@ def tile_list_roundabout_entry_scores_kernel(
 
             nc.vector.memset(tab_planes[:].bitcast(I32), 0)
             nc.vector.memset(w4_plane[:].bitcast(I32), 0)
+            def load_w1(a):
+                nc.sync.dma_start(out=w1_raw[a][:], in_=w1[512 * a : 512 * (a + 1), :].rearrange("(p j) c -> p j c", j=PACK))
+
+            load_w1(0)
+            load_w1(1)
             for q in range(4):
-                nc.gpsimd.dma_start(
+                nc.sync.dma_start(
                     out=tab_planes[32 * q : 32 * q + 4 * PASSES, :].bitcast(I32),
                     in_=tab_scales[:, 4 * q : 4 * q + 4, :].bitcast(I32),
                 )
-            for a in range(PASSES):
-                nc.sync.dma_start(out=w1_raw[a][:], in_=w1[512 * a : 512 * (a + 1), :].rearrange("(p j) c -> p j c", j=PACK))
             nc.sync.dma_start(idx[:], offs)
+            load_w1(2)
             for a in range(PASSES):
                 nc.sync.dma_start(
                     out=tab_sb[a][:].bitcast(I32), in_=tab_words[a].rearrange("p t i -> p (t i)").bitcast(I32)
                 )
             nc.sync.dma_start(out=gain_sb[:], in_=gain.rearrange("(p t) -> p t", t=PACK))
             nc.sync.dma_start(idx2[:], offs2)
-            for t in range(PACK):
-                load_slice(t)
+            for t, j0, n in pieces:
+                load_wgs(t, j0, n)
+                if j0 == 0:
+                    load_page(t)
             nc.sync.dma_start(idx3[:], offs3)
             nc.sync.dma_start(idx4[:], offs4)
             nc.sync.dma_start(out=conf_sb[:], in_=conf.rearrange("(p t) -> p t", t=PACK))
@@ -90,7 +107,7 @@ def tile_list_roundabout_entry_scores_kernel(
                 )
 
             for a in range(PASSES):
-                nc.scalar.copy(
+                nc.vector.tensor_copy(
                     out=w1_bf[a][:].rearrange("p (t m j) -> p m t j", t=PACK, j=PACK),
                     in_=w1_raw[a][:].rearrange("p j (m t) -> p m t j", t=PACK),
                 )
@@ -107,10 +124,16 @@ def tile_list_roundabout_entry_scores_kernel(
                 )
 
         with tc.tile_pool(name="tail", bufs=1) as tail:
-            for t in range(PACK):
-                for u in range(2):
-                    cols = slice(HALF * u, HALF * (u + 1))
-                    x = psum.tile([P, BANK], F32, name="bank")
+            for t, j0, n in pieces:
+                if (t, j0) == (0, 0):
+                    nc.vector.tensor_scalar(weight[t, j0][:], wgs_sb[t, j0][:], gain_sb[:, t : t + 1], None, ALU.mult)
+                    act = keep.tile([P, n], F32, name="act_first")
+                else:
+                    nc.scalar.activation(weight[t, j0][:], wgs_sb[t, j0][:], ACT.Copy, scale=gain_sb[:, t : t + 1])
+                    act = wgs_sb[t, j0]
+                for j in range(j0, j0 + n, HALF):
+                    cols = slice(j, j + HALF)
+                    x = psum.tile([P, BANK], F32, name="x", bufs=2)
                     for a in range(PASSES):
                         nc.tensor.matmul_mx(
                             out=x[:],
@@ -121,23 +144,17 @@ def tile_list_roundabout_entry_scores_kernel(
                             start=(a == 0),
                             stop=(a == PASSES - 1),
                         )
-                    act = tail.tile([P, HALF], F32, name="act", bufs=2)
-                    nc.scalar.activation(act[:], x[:], ACT.Silu)
-                    nc.scalar.activation(h[t][:, cols], act[:], ACT.Copy, scale=gain_sb[:, t : t + 1])
-                    if t == 0:
-                        nc.vector.tensor_tensor(
-                            pages[t][:].indirect(idx2[:, 32 * u : 32 * (u + 1)]), h[t][:, cols], wgs_sb[t][:, cols], ALU.mult
-                        )
-                if t > 0:
-                    nc.vector.tensor_tensor(pages[t][:].indirect(idx2[:]), h[t][:], wgs_sb[t][:], ALU.mult)
+                    nc.scalar.activation(act[:, j - j0 : j - j0 + HALF], x[:], ACT.Silu)
+                nc.vector.tensor_tensor(
+                    pages[t][:].indirect(idx2[:, j0 // 16 : (j0 + n) // 16]), act[:], weight[t, j0][:], ALU.mult
+                )
 
             arm_a = [tail.tile([P, PAIRS], F32, name=f"arm_a{t}") for t in range(PACK)]
             arm_b = [tail.tile([P, PAIRS], F32, name=f"arm_b{t}") for t in range(PACK)]
-            diff = [tail.tile([P, PAIRS], F32, name=f"diff{t}") for t in range(PACK)]
             gap = [tail.tile([P, PAIRS], F32, name=f"gap{t}") for t in range(PACK)]
-            neg_gap = [tail.tile([P, PAIRS], F32, name=f"neg_gap{t}") for t in range(PACK)]
+            abs_t = [tail.tile([P, PAIRS], F32, name=f"abs_t{t}") for t in range(PACK)]
+            neg_gap = [abs_t[(t + 1) % PACK] for t in range(PACK)]
             starts = [sum(CHUNKS[:c]) for c in range(len(CHUNKS))]
-            b_rows = [tail.tile([P, PACK, w], BF16, name=f"b_rows{c}", align_bytes=64) for c, w in enumerate(CHUNKS)]
 
             def fetch_a(t):
                 nc.vector.tensor_copy(arm_a[t][:], pages[t][:].indirect(idx3[:]))
@@ -146,8 +163,21 @@ def tile_list_roundabout_entry_scores_kernel(
                 nc.vector.tensor_copy(arm_b[t][:], pages[t][:].indirect(idx4[:]))
 
             def gaps(t):
-                nc.vector.tensor_tensor(diff[t][:], arm_a[t][:], arm_b[t][:], ALU.subtract)
-                nc.scalar.activation(gap[t][:], diff[t][:], ACT.Abs, scale=conf_sb[:, t : t + 1])
+                neg_b = tail.tile([P, PAIRS], F32, name="neg_b", tag="work")
+                nc.scalar.activation(neg_b[:], arm_b[t][:], ACT.Copy, scale=-1.0)
+                diff_t = psum.tile([P, BANK], F32, name="y", bufs=6)
+                for m in range(PAIRS // P):
+                    cols = slice(P * m, P * (m + 1))
+                    nc.tensor.matmul(diff_t[:, cols], arm_a[t][:, cols], ident[:], start=True, stop=False, is_transpose=True)
+                    nc.tensor.matmul(diff_t[:, cols], neg_b[:, cols], ident[:], start=False, stop=True, is_transpose=True)
+                nc.scalar.activation(abs_t[t][:], diff_t[:], ACT.Abs)
+                dist = psum.tile([P, BANK], F32, name="y", bufs=6)
+                for m in range(PAIRS // P):
+                    cols = slice(P * m, P * (m + 1))
+                    nc.tensor.transpose(dist[:, cols], abs_t[t][:, cols], ident[:])
+                nc.scalar.activation(gap[t][:], dist[:], ACT.Copy, scale=conf_sb[:, t : t + 1])
+
+            def negate_gap(t):
                 nc.scalar.activation(neg_gap[t][:], gap[t][:], ACT.Copy, scale=-1.0)
 
             def put_a(t):
@@ -156,44 +186,32 @@ def tile_list_roundabout_entry_scores_kernel(
             def put_b(t):
                 nc.vector.tensor_tensor(pages[t][:].indirect(idx4[:]), arm_b[t][:], neg_gap[t][:], ALU.add)
 
-            def round_slot(t, c):
-                nc.scalar.copy(out=b_rows[c][:, t, :], in_=pages[t][:, starts[c] : starts[c] + CHUNKS[c]])
-
             def round_slice(t):
-                for c in range(len(CHUNKS)):
-                    round_slot(t, c)
+                spans = zip(starts, CHUNKS) if t == PACK - 1 else [(0, T2)]
+                for c0, w in spans:
+                    nc.scalar.copy(out=b_rows[:, t, c0 : c0 + w], in_=pages[t][:, c0 : c0 + w])
 
-            fetch_a(0)
-            fetch_b(0)
-            fetch_a(1)
-            gaps(0)
-            fetch_b(1)
-            fetch_a(2)
-            put_a(0)
-            gaps(1)
-            put_b(0)
-            fetch_b(2)
-            put_a(1)
-            gaps(2)
-            round_slice(0)
-            put_b(1)
-            fetch_a(3)
-            fetch_b(3)
-            put_a(2)
-            gaps(3)
-            round_slice(1)
-            put_b(2)
-            round_slice(2)
-            put_a(3)
-            put_b(3)
-            round_slice(3)
+            for t in range(PACK):
+                fetch_a(t)
+                fetch_b(t)
+                gaps(t)
+                if t > 0:
+                    negate_gap(t - 1)
+            negate_gap(PACK - 1)
+            b_rows = tail.tile([P, PACK, T2], BF16, name="b_rows", tag="work")
+            for t in range(PACK + 1):
+                if t < PACK:
+                    put_a(t)
+                if t > 0:
+                    put_b(t - 1)
+                    round_slice(t - 1)
 
             out_blocks = out.rearrange("(b p) c -> p b c", p=P)
             for c, w in enumerate(CHUNKS):
                 b_bf = tail.tile([P, w, PACK], BF16, name=f"b_bf{c}", align_bytes=64)
                 nc.vector.tensor_copy(
                     out=b_bf[:].rearrange("p (c i) t -> p c t i", i=4),
-                    in_=b_rows[c][:].rearrange("p t (c i) -> p c t i", i=4),
+                    in_=b_rows[:, :, starts[c] : starts[c] + w].rearrange("p t (c i) -> p c t i", i=4),
                 )
                 b_codes = tail.tile([P, w], U32, name=f"b_codes{c}", align_bytes=64)
                 b_plane = tail.tile([P, w], U8, name=f"b_plane{c}", align_bytes=64)
@@ -204,7 +222,7 @@ def tile_list_roundabout_entry_scores_kernel(
                 for g in range(N // P // 2):
                     staged = tail.tile([P, 2, w], F32, name="staged", bufs=6)
                     for s in range(2 // per_bank):
-                        y = psum.tile([P, per_bank, w], F32, name="bank")
+                        y = psum.tile([P, per_bank, w], F32, name="y", bufs=6)
                         for i in range(per_bank):
                             b = 2 * g + per_bank * s + i
                             nc.tensor.matmul_mx(

@@ -44,17 +44,16 @@ def tile_list_roundabout_entry_scores_kernel(
         pages = [keep.tile([P, T2], F32, name=f"page{t}") for t in range(PACK)]
         pieces = [(0, 0, HALF), (0, HALF, HALF)] + [(t, 0, S) for t in range(1, PACK)]
         wgs_sb = {(t, j0): keep.tile([P, n], F32, name=f"wgs{t}_{j0}") for t, j0, n in pieces}
-        weight = {(t, j0): keep.tile([P, n], F32, name=f"weight{t}_{j0}") for t, j0, n in pieces}
+        h = {(t, j0): keep.tile([P, n], F32, name=f"h{t}_{j0}") for t, j0, n in pieces}
         w4_codes = keep.tile([P, 2 * N], U8, name="w4_codes", align_bytes=64)
         w4_plane = keep.tile([P, N], U8, name="w4_plane", align_bytes=64)
-        v_codes = [keep.tile([P, S], U32, name=f"v_codes{a}", align_bytes=64) for a in range(PASSES - 1)]
-        tab_planes = keep.tile([P, T], U8, name="tab_planes", tag="planes_then_codes", align_bytes=64)
-        v_planes = keep.tile([P, S], U8, name="v_planes", align_bytes=64)
+        tab_planes = keep.tile([P, T], U8, name="tab_planes", tag="v1", align_bytes=64)
+        tab_last = keep.tile([P, T], U32, name="tab_last", tag="tab_last", align_bytes=64)
+        w1_bf_last = keep.tile([P, PACK * H], BF16, name="w1_bf_last", tag="w1_bf_last", align_bytes=64)
         w1_codes = [keep.tile([P, H], U32, name=f"w1_codes{a}", align_bytes=64) for a in range(PASSES)]
         w1_plane = [keep.tile([P, H], U8, name=f"w1_plane{a}", align_bytes=64) for a in range(PASSES)]
 
         ident = keep.tile([P, P], F32, name="ident")
-        make_identity(nc, ident[:])
 
         def load_wgs(t, j0, n):
             for q in range(4):
@@ -68,24 +67,24 @@ def tile_list_roundabout_entry_scores_kernel(
 
 
         with tc.tile_pool(name="head", bufs=1) as head:
-            tab_sb = [head.tile([P, T], U32, name=f"tab{a}", align_bytes=64) for a in range(PASSES)]
+            tab_sb = [head.tile([P, T], U32, name=f"tab{a}", align_bytes=64) for a in range(PASSES - 1)] + [tab_last]
             w1_raw = [head.tile([P, PACK, H], F32, name=f"w1_raw{a}") for a in range(PASSES)]
-            w1_bf = [head.tile([P, PACK * H], BF16, name=f"w1_bf{a}", align_bytes=64) for a in range(PASSES)]
+            w1_bf = [head.tile([P, PACK * H], BF16, name=f"w1_bf{a}", align_bytes=64) for a in range(PASSES - 1)] + [w1_bf_last]
 
             nc.vector.memset(tab_planes[:].bitcast(I32), 0)
             nc.vector.memset(w4_plane[:].bitcast(I32), 0)
             def load_w1(a):
                 nc.sync.dma_start(out=w1_raw[a][:], in_=w1[512 * a : 512 * (a + 1), :].rearrange("(p j) c -> p j c", j=PACK))
 
-            load_w1(0)
-            load_w1(1)
             for q in range(4):
-                nc.sync.dma_start(
+                nc.gpsimd.dma_start(
                     out=tab_planes[32 * q : 32 * q + 4 * PASSES, :].bitcast(I32),
                     in_=tab_scales[:, 4 * q : 4 * q + 4, :].bitcast(I32),
                 )
+            make_identity(nc, ident[:])
+            for a in range(PASSES):
+                load_w1(a)
             nc.sync.dma_start(idx[:], offs)
-            load_w1(2)
             for a in range(PASSES):
                 nc.sync.dma_start(
                     out=tab_sb[a][:].bitcast(I32), in_=tab_words[a].rearrange("p t i -> p (t i)").bitcast(I32)
@@ -113,10 +112,11 @@ def tile_list_roundabout_entry_scores_kernel(
                 )
                 nc.vector.quantize_mx(out=w1_codes[a][:].bitcast(FP8X4), scales=w1_plane[a][:], in_=w1_bf[a][:])
 
+            v_planes = keep.tile([P, S], U8, name="v_planes", tag="w1_bf_last", align_bytes=64)
             nc.vector.tensor_copy(v_planes[:], tab_planes[:].indirect(idx[:]))
+            v_codes = [keep.tile([P, S], U32, name=f"v_codes{a}", tag=f"v{a}", align_bytes=64) for a in range(PASSES)]
             for a in range(PASSES - 1):
                 nc.vector.tensor_copy(v_codes[a][:], tab_sb[a][:].indirect(idx[:]))
-            v_codes.append(keep.tile([P, S], U32, name="v_codes_last", tag="planes_then_codes", align_bytes=64))
             for u in range(2):
                 nc.vector.tensor_copy(
                     v_codes[PASSES - 1][:, HALF * u : HALF * (u + 1)],
@@ -125,12 +125,11 @@ def tile_list_roundabout_entry_scores_kernel(
 
         with tc.tile_pool(name="tail", bufs=1) as tail:
             for t, j0, n in pieces:
-                if (t, j0) == (0, 0):
-                    nc.vector.tensor_scalar(weight[t, j0][:], wgs_sb[t, j0][:], gain_sb[:, t : t + 1], None, ALU.mult)
-                    act = keep.tile([P, n], F32, name="act_first")
-                else:
-                    nc.scalar.activation(weight[t, j0][:], wgs_sb[t, j0][:], ACT.Copy, scale=gain_sb[:, t : t + 1])
-                    act = wgs_sb[t, j0]
+                first = (t, j0) == (0, 0)
+                weight = wgs_sb[t, j0]
+                if first:
+                    weight = keep.tile([P, n], F32, name="weight_first", tag="tab_last", align_bytes=64)
+                    nc.vector.tensor_scalar(weight[:], wgs_sb[t, j0][:], gain_sb[:, t : t + 1], None, ALU.mult)
                 for j in range(j0, j0 + n, HALF):
                     cols = slice(j, j + HALF)
                     x = psum.tile([P, BANK], F32, name="x", bufs=2)
@@ -144,13 +143,17 @@ def tile_list_roundabout_entry_scores_kernel(
                             start=(a == 0),
                             stop=(a == PASSES - 1),
                         )
-                    nc.scalar.activation(act[:, j - j0 : j - j0 + HALF], x[:], ACT.Silu)
+                    part = h[t, j0][:, j - j0 : j - j0 + HALF]
+                    nc.scalar.activation(part, x[:], ACT.Silu)
+                    if not first:
+                        nc.scalar.activation(part, part, ACT.Copy, scale=gain_sb[:, t : t + 1])
                 nc.vector.tensor_tensor(
-                    pages[t][:].indirect(idx2[:, j0 // 16 : (j0 + n) // 16]), act[:], weight[t, j0][:], ALU.mult
+                    pages[t][:].indirect(idx2[:, j0 // 16 : (j0 + n) // 16]), h[t, j0][:], weight[:], ALU.mult
                 )
 
-            arm_a = [tail.tile([P, PAIRS], F32, name=f"arm_a{t}") for t in range(PACK)]
-            arm_b = [tail.tile([P, PAIRS], F32, name=f"arm_b{t}") for t in range(PACK)]
+            arms = [keep.tile([P, 2, PAIRS], F32, name=f"arms{t}", tag=f"v{t}", align_bytes=64) for t in range(PACK)]
+            arm_a = [arms[t][:, 0, :] for t in range(PACK)]
+            arm_b = [arms[t][:, 1, :] for t in range(PACK)]
             gap = [tail.tile([P, PAIRS], F32, name=f"gap{t}") for t in range(PACK)]
             abs_t = [tail.tile([P, PAIRS], F32, name=f"abs_t{t}") for t in range(PACK)]
             neg_gap = [abs_t[(t + 1) % PACK] for t in range(PACK)]

@@ -56,7 +56,7 @@ def tile_list_roundabout_entry_scores_kernel(
         ident = keep.tile([P, P], F32, name="ident")
 
         def load_wgs(t, j0, n):
-            for q in range(4):
+            for q in (0, 2, 1, 3):
                 nc.sync.dma_start(
                     out=wgs_sb[t, j0][32 * q : 32 * q + 32, :],
                     in_=wgs.rearrange("(q t) j -> t q j", t=PACK)[t][:, j0 : j0 + n],
@@ -106,9 +106,10 @@ def tile_list_roundabout_entry_scores_kernel(
                 )
 
             for a in range(PASSES):
-                nc.vector.tensor_copy(
-                    out=w1_bf[a][:].rearrange("p (t m j) -> p m t j", t=PACK, j=PACK),
-                    in_=w1_raw[a][:].rearrange("p j (m t) -> p m t j", t=PACK),
+                deal = nc.vector.tensor_copy if a == PASSES - 1 else nc.scalar.copy
+                deal(
+                    out=w1_bf[a][:].rearrange("p (t m j) -> p m j t", t=PACK, j=PACK),
+                    in_=w1_raw[a][:].rearrange("p j (m t) -> p m j t", t=PACK),
                 )
                 nc.vector.quantize_mx(out=w1_codes[a][:].bitcast(FP8X4), scales=w1_plane[a][:], in_=w1_bf[a][:])
 

@@ -211,7 +211,9 @@ def tile_list_roundabout_entry_scores_kernel(
                     round_slice(t - 1)
 
             out_blocks = out.rearrange("(b p) c -> p b c", p=P)
-            for c, w in enumerate(CHUNKS):
+
+            def quantise(c):
+                w = CHUNKS[c]
                 b_bf = tail.tile([P, w, PACK], BF16, name=f"b_bf{c}", align_bytes=64)
                 nc.vector.tensor_copy(
                     out=b_bf[:].rearrange("p (c i) t -> p c t i", i=4),
@@ -222,28 +224,45 @@ def tile_list_roundabout_entry_scores_kernel(
                 nc.vector.quantize_mx(
                     out=b_codes[:].bitcast(FP8X4), scales=b_plane[:], in_=b_bf[:].rearrange("p w t -> p (w t)")
                 )
-                per_bank = BANK // w
-                for g in range(N // P // 2):
+                return b_codes, b_plane
+
+            def scores(y, b, operand):
+                nc.tensor.matmul_mx(
+                    out=y,
+                    lhsT=w4_codes[:, 2 * P * b : 2 * P * (b + 1)].bitcast(FP4X4),
+                    lhsT_scale=w4_plane[:, P * b : P * (b + 1)],
+                    rhs=operand[0][:].bitcast(FP8X4),
+                    rhs_scale=operand[1][:],
+                    start=True,
+                    stop=True,
+                )
+
+            for c in range(2):
+                w = CHUNKS[c]
+                operand = quantise(c)
+                for b in range(0, N // P, 2):
+                    y = psum.tile([P, 2, w], F32, name="y", bufs=6)
+                    for i in range(2):
+                        scores(y[:, i, :], b + i, operand)
                     staged = tail.tile([P, 2, w], F32, name="staged", bufs=6)
-                    for s in range(2 // per_bank):
-                        y = psum.tile([P, per_bank, w], F32, name="y", bufs=6)
-                        for i in range(per_bank):
-                            b = 2 * g + per_bank * s + i
-                            nc.tensor.matmul_mx(
-                                out=y[:, i, :],
-                                lhsT=w4_codes[:, 2 * P * b : 2 * P * (b + 1)].bitcast(FP4X4),
-                                lhsT_scale=w4_plane[:, P * b : P * (b + 1)],
-                                rhs=b_codes[:].bitcast(FP8X4),
-                                rhs_scale=b_plane[:],
-                                start=True,
-                                stop=True,
-                            )
-                        dst = staged[:, per_bank * s : per_bank * (s + 1), :]
-                        bank_no = g * (2 // per_bank) + s
-                        if c >= len(CHUNKS) - 2 and bank_no % 2 == 1:
-                            nc.vector.tensor_copy(out=dst, in_=y[:])
-                        else:
-                            nc.scalar.copy(out=dst, in_=y[:])
-                    nc.sync.dma_start(
-                        out=out_blocks[:, 2 * g : 2 * g + 2, starts[c] : starts[c] + w], in_=staged[:]
-                    )
+                    nc.scalar.copy(out=staged[:], in_=y[:])
+                    nc.sync.dma_start(out=out_blocks[:, b : b + 2, starts[c] : starts[c] + w], in_=staged[:])
+
+            def two_banks(jobs, dst):
+                staged = tail.tile([P, 2, BANK], F32, name="staged", bufs=6)
+                for i, (b, operand) in enumerate(jobs):
+                    y = psum.tile([P, BANK], F32, name="y", bufs=6)
+                    scores(y[:], b, operand)
+                    empty = nc.vector.tensor_copy if i else nc.scalar.copy
+                    empty(out=staged[:, i, :], in_=y[:])
+                nc.sync.dma_start(out=dst, in_=staged[:])
+
+            left, right = quantise(2), quantise(3)
+            for b in range(N // P):
+                two_banks(
+                    [(b, left), (b, right)],
+                    out_blocks[:, b, starts[2] : starts[4]].rearrange("p (i c) -> p i c", i=2),
+                )
+            last = quantise(4)
+            for b in range(0, N // P, 2):
+                two_banks([(b, last), (b + 1, last)], out_blocks[:, b : b + 2, starts[4] :])

from contextlib import ExitStack

import concourse.mybir as mybir
from concourse.masks import make_identity

K, T, S, H, T2, PAIRS, N = 1536, 4096, 1024, 512, 2048, 512, 768
FLOPS = 2 * K * H * S + 2 * H * N * T2

F32 = mybir.dt.float32
BF16 = mybir.dt.bfloat16
I32 = mybir.dt.int32
U32 = mybir.dt.uint32
U16 = mybir.dt.uint16
U8 = mybir.dt.uint8
FP8X4 = mybir.dt.float8_e4m3fn_x4
FP4X4 = mybir.dt.float4_e2m1fn_x4
ALU = mybir.AluOpType
ACT = mybir.ActivationFunctionType

P = 128
PACK = 4
PASSES = K // (P * PACK)
HALF = S // 2
CHUNKS = [256, 256, 512, 512, 512]
BANK = 512


def tile_list_roundabout_entry_scores_kernel(
    tc, tab_words, tab_scales, w1, gain, wgs, page0, conf, w4_words, w4_scales, offs, offs2, offs3, offs4, out
):
    nc = tc.nc
    with ExitStack() as ctx:
        lists = ctx.enter_context(tc.tile_pool(name="lists", bufs=1))
        keep = ctx.enter_context(tc.tile_pool(name="keep", bufs=1))
        psum = ctx.enter_context(tc.psum_pool(name="psum", bufs=1))

        idx = lists.tile([P, S // 16], U16, name="idx")
        idx2 = lists.tile([P, S // 16], U16, name="idx2")
        idx3 = lists.tile([P, PAIRS // 16], U16, name="idx3")
        idx4 = lists.tile([P, PAIRS // 16], U16, name="idx4")

        gain_sb = keep.tile([P, PACK], F32, name="gain_sb")
        conf_sb = keep.tile([P, PACK], F32, name="conf_sb")
        pages = [keep.tile([P, T2], F32, name=f"page{t}") for t in range(PACK)]
        pieces = [(0, 0, HALF), (0, HALF, HALF)] + [(t, 0, S) for t in range(1, PACK)]
        wgs_sb = {(t, j0): keep.tile([P, n], F32, name=f"wgs{t}_{j0}") for t, j0, n in pieces}
        h = {(t, j0): keep.tile([P, n], F32, name=f"h{t}_{j0}") for t, j0, n in pieces}
        w4_codes = keep.tile([P, 2 * N], U8, name="w4_codes", align_bytes=64)
        w4_plane = keep.tile([P, N], U8, name="w4_plane", align_bytes=64)
        tab_planes = keep.tile([P, T], U8, name="tab_planes", tag="v1", align_bytes=64)
        tab_last = keep.tile([P, T], U32, name="tab_last", tag="tab_last", align_bytes=64)
        w1_bf_last = keep.tile([P, PACK * H], BF16, name="w1_bf_last", tag="w1_bf_last", align_bytes=64)
        w1_codes = [keep.tile([P, H], U32, name=f"w1_codes{a}", align_bytes=64) for a in range(PASSES)]
        w1_plane = [keep.tile([P, H], U8, name=f"w1_plane{a}", align_bytes=64) for a in range(PASSES)]

        ident = keep.tile([P, P], F32, name="ident")

        def load_wgs(t, j0, n):
            for q in (0, 2, 1, 3):
                nc.sync.dma_start(
                    out=wgs_sb[t, j0][32 * q : 32 * q + 32, :],
                    in_=wgs.rearrange("(q t) j -> t q j", t=PACK)[t][:, j0 : j0 + n],
                )

        def load_page(t):
            nc.sync.dma_start(out=pages[t][:], in_=page0.rearrange("(p t) c -> t p c", t=PACK)[t])


        with tc.tile_pool(name="head", bufs=1) as head:
            tab_sb = [head.tile([P, T], U32, name=f"tab{a}", align_bytes=64) for a in range(PASSES - 1)] + [tab_last]
            w1_raw = [head.tile([P, PACK, H], F32, name=f"w1_raw{a}") for a in range(PASSES)]
            w1_bf = [head.tile([P, PACK * H], BF16, name=f"w1_bf{a}", align_bytes=64) for a in range(PASSES - 1)] + [w1_bf_last]

            nc.vector.memset(tab_planes[:].bitcast(I32), 0)
            nc.vector.memset(w4_plane[:].bitcast(I32), 0)
            def load_w1(a):
                nc.sync.dma_start(out=w1_raw[a][:], in_=w1[512 * a : 512 * (a + 1), :].rearrange("(p j) c -> p j c", j=PACK))

            for q in range(4):
                nc.gpsimd.dma_start(
                    out=tab_planes[32 * q : 32 * q + 4 * PASSES, :].bitcast(I32),
                    in_=tab_scales[:, 4 * q : 4 * q + 4, :].bitcast(I32),
                )
            make_identity(nc, ident[:])
            for a in range(PASSES):
                load_w1(a)
            nc.sync.dma_start(idx[:], offs)
            for a in range(PASSES):
                nc.sync.dma_start(
                    out=tab_sb[a][:].bitcast(I32), in_=tab_words[a].rearrange("p t i -> p (t i)").bitcast(I32)
                )
            nc.sync.dma_start(out=gain_sb[:], in_=gain.rearrange("(p t) -> p t", t=PACK))
            nc.sync.dma_start(idx2[:], offs2)
            for t, j0, n in pieces:
                load_wgs(t, j0, n)
                if j0 == 0:
                    load_page(t)
            nc.sync.dma_start(idx3[:], offs3)
            nc.sync.dma_start(idx4[:], offs4)
            nc.sync.dma_start(out=conf_sb[:], in_=conf.rearrange("(p t) -> p t", t=PACK))
            nc.sync.dma_start(out=w4_codes[:].bitcast(I32), in_=w4_words[0].bitcast(I32))
            for q in range(4):
                nc.sync.dma_start(
                    out=w4_plane[32 * q : 32 * q + 4, :].bitcast(I32),
                    in_=w4_scales[0, 4 * q : 4 * q + 4, :].bitcast(I32),
                )

            for a in range(PASSES):
                deal = nc.vector.tensor_copy if a == PASSES - 1 else nc.scalar.copy
                deal(
                    out=w1_bf[a][:].rearrange("p (t m j) -> p m j t", t=PACK, j=PACK),
                    in_=w1_raw[a][:].rearrange("p j (m t) -> p m j t", t=PACK),
                )
                nc.vector.quantize_mx(out=w1_codes[a][:].bitcast(FP8X4), scales=w1_plane[a][:], in_=w1_bf[a][:])

            v_planes = keep.tile([P, S], U8, name="v_planes", tag="w1_bf_last", align_bytes=64)
            nc.vector.tensor_copy(v_planes[:], tab_planes[:].indirect(idx[:]))
            v_codes = [keep.tile([P, S], U32, name=f"v_codes{a}", tag=f"v{a}", align_bytes=64) for a in range(PASSES)]
            for a in range(PASSES - 1):
                nc.vector.tensor_copy(v_codes[a][:], tab_sb[a][:].indirect(idx[:]))
            for u in range(2):
                nc.vector.tensor_copy(
                    v_codes[PASSES - 1][:, HALF * u : HALF * (u + 1)],
                    tab_sb[PASSES - 1][:].indirect(idx[:, 32 * u : 32 * (u + 1)]),
                )

        with tc.tile_pool(name="tail", bufs=1) as tail:
            for t, j0, n in pieces:
                first = (t, j0) == (0, 0)
                weight = wgs_sb[t, j0]
                if first:
                    weight = keep.tile([P, n], F32, name="weight_first", tag="tab_last", align_bytes=64)
                    nc.vector.tensor_scalar(weight[:], wgs_sb[t, j0][:], gain_sb[:, t : t + 1], None, ALU.mult)
                for j in range(j0, j0 + n, HALF):
                    cols = slice(j, j + HALF)
                    x = psum.tile([P, BANK], F32, name="x", bufs=2)
                    for a in range(PASSES):
                        nc.tensor.matmul_mx(
                            out=x[:],
                            lhsT=w1_codes[a][:, P * t : P * (t + 1)].bitcast(FP8X4),
                            lhsT_scale=w1_plane[a][:, P * t : P * (t + 1)],
                            rhs=v_codes[a][:, cols].bitcast(FP8X4),
                            rhs_scale=v_planes[4 * a :, cols],
                            start=(a == 0),
                            stop=(a == PASSES - 1),
                        )
                    part = h[t, j0][:, j - j0 : j - j0 + HALF]
                    nc.scalar.activation(part, x[:], ACT.Silu)
                    if not first:
                        nc.scalar.activation(part, part, ACT.Copy, scale=gain_sb[:, t : t + 1])
                nc.vector.tensor_tensor(
                    pages[t][:].indirect(idx2[:, j0 // 16 : (j0 + n) // 16]), h[t, j0][:], weight[:], ALU.mult
                )

            arms = [keep.tile([P, 2, PAIRS], F32, name=f"arms{t}", tag=f"v{t}", align_bytes=64) for t in range(PACK)]
            arm_a = [arms[t][:, 0, :] for t in range(PACK)]
            arm_b = [arms[t][:, 1, :] for t in range(PACK)]
            gap = [tail.tile([P, PAIRS], F32, name=f"gap{t}") for t in range(PACK)]
            abs_t = [tail.tile([P, PAIRS], F32, name=f"abs_t{t}") for t in range(PACK)]
            neg_gap = [abs_t[(t + 1) % PACK] for t in range(PACK)]
            starts = [sum(CHUNKS[:c]) for c in range(len(CHUNKS))]

            def fetch_a(t):
                nc.vector.tensor_copy(arm_a[t][:], pages[t][:].indirect(idx3[:]))

            def fetch_b(t):
                nc.vector.tensor_copy(arm_b[t][:], pages[t][:].indirect(idx4[:]))

            def gaps(t):
                neg_b = tail.tile([P, PAIRS], F32, name="neg_b", tag="work")
                nc.scalar.activation(neg_b[:], arm_b[t][:], ACT.Copy, scale=-1.0)
                diff_t = psum.tile([P, BANK], F32, name="y", bufs=6)
                for m in range(PAIRS // P):
                    cols = slice(P * m, P * (m + 1))
                    nc.tensor.matmul(diff_t[:, cols], arm_a[t][:, cols], ident[:], start=True, stop=False, is_transpose=True)
                    nc.tensor.matmul(diff_t[:, cols], neg_b[:, cols], ident[:], start=False, stop=True, is_transpose=True)
                nc.scalar.activation(abs_t[t][:], diff_t[:], ACT.Abs)
                dist = psum.tile([P, BANK], F32, name="y", bufs=6)
                for m in range(PAIRS // P):
                    cols = slice(P * m, P * (m + 1))
                    nc.tensor.transpose(dist[:, cols], abs_t[t][:, cols], ident[:])
                nc.scalar.activation(gap[t][:], dist[:], ACT.Copy, scale=conf_sb[:, t : t + 1])

            def negate_gap(t):
                nc.scalar.activation(neg_gap[t][:], gap[t][:], ACT.Copy, scale=-1.0)

            def put_a(t):
                nc.vector.tensor_tensor(pages[t][:].indirect(idx3[:]), arm_a[t][:], gap[t][:], ALU.add)

            def put_b(t):
                nc.vector.tensor_tensor(pages[t][:].indirect(idx4[:]), arm_b[t][:], neg_gap[t][:], ALU.add)

            def round_slice(t):
                spans = zip(starts, CHUNKS) if t == PACK - 1 else [(0, T2)]
                for c0, w in spans:
                    nc.scalar.copy(out=b_rows[:, t, c0 : c0 + w], in_=pages[t][:, c0 : c0 + w])

            for t in range(PACK):
                fetch_a(t)
                fetch_b(t)
                gaps(t)
                if t > 0:
                    negate_gap(t - 1)
            negate_gap(PACK - 1)
            b_rows = tail.tile([P, PACK, T2], BF16, name="b_rows", tag="work")
            for t in range(PACK + 1):
                if t < PACK:
                    put_a(t)
                if t > 0:
                    put_b(t - 1)
                    round_slice(t - 1)

            out_blocks = out.rearrange("(b p) c -> p b c", p=P)

            def quantise(c):
                w = CHUNKS[c]
                b_bf = tail.tile([P, w, PACK], BF16, name=f"b_bf{c}", align_bytes=64)
                nc.vector.tensor_copy(
                    out=b_bf[:].rearrange("p (c i) t -> p c t i", i=4),
                    in_=b_rows[:, :, starts[c] : starts[c] + w].rearrange("p t (c i) -> p c t i", i=4),
                )
                b_codes = tail.tile([P, w], U32, name=f"b_codes{c}", align_bytes=64)
                b_plane = tail.tile([P, w], U8, name=f"b_plane{c}", align_bytes=64)
                nc.vector.quantize_mx(
                    out=b_codes[:].bitcast(FP8X4), scales=b_plane[:], in_=b_bf[:].rearrange("p w t -> p (w t)")
                )
                return b_codes, b_plane

            def scores(y, b, operand):
                nc.tensor.matmul_mx(
                    out=y,
                    lhsT=w4_codes[:, 2 * P * b : 2 * P * (b + 1)].bitcast(FP4X4),
                    lhsT_scale=w4_plane[:, P * b : P * (b + 1)],
                    rhs=operand[0][:].bitcast(FP8X4),
                    rhs_scale=operand[1][:],
                    start=True,
                    stop=True,
                )

            for c in range(2):
                w = CHUNKS[c]
                operand = quantise(c)
                for b in range(0, N // P, 2):
                    y = psum.tile([P, 2, w], F32, name="y", bufs=6)
                    for i in range(2):
                        scores(y[:, i, :], b + i, operand)
                    staged = tail.tile([P, 2, w], F32, name="staged", bufs=6)
                    nc.scalar.copy(out=staged[:], in_=y[:])
                    nc.sync.dma_start(out=out_blocks[:, b : b + 2, starts[c] : starts[c] + w], in_=staged[:])

            def two_banks(jobs, dst):
                staged = tail.tile([P, 2, BANK], F32, name="staged", bufs=6)
                for i, (b, operand) in enumerate(jobs):
                    y = psum.tile([P, BANK], F32, name="y", bufs=6)
                    scores(y[:], b, operand)
                    empty = nc.vector.tensor_copy if i else nc.scalar.copy
                    empty(out=staged[:, i, :], in_=y[:])
                nc.sync.dma_start(out=dst, in_=staged[:])

            left, right = quantise(2), quantise(3)
            for b in range(N // P):
                two_banks(
                    [(b, left), (b, right)],
                    out_blocks[:, b, starts[2] : starts[4]].rearrange("p (i c) -> p i c", i=2),
                )
            last = quantise(4)
            for b in range(0, N // P, 2):
                two_banks([(b, last), (b + 1, last)], out_blocks[:, b : b + 2, starts[4] :])
